import numpy as np, ml_dtypes
CORES = [1,5,17,21,33,37,49,53]
N = 8
import mx_ref
BF = ml_dtypes.bfloat16
def gentries(a):
    return np.ascontiguousarray(a.reshape(8, 16, -1).transpose(0, 2, 1)).reshape(8, -1)
def gtable(e):
    e = np.asarray(e); return np.ascontiguousarray(e.reshape(8, -1, 16).transpose(0, 2, 1)).reshape(128, -1).astype(np.int32)
def gcols(t, e):
    v = np.concatenate([t.reshape(8, 16, -1, 4), np.zeros((8, 16, 1, 4), BF)], axis=2)
    return np.ascontiguousarray(np.stack([v[g][:, e[g]] for g in range(8)])).reshape(128, -1)
def tile(rs):
    return np.stack(rs, axis=2).reshape(128, -1).astype(BF)
def pick(q, e):
    c = np.concatenate([q[0].reshape(128, -1, 4), np.zeros((128, 1, 4), np.uint8)], axis=1); s = np.concatenate([q[1], np.ones((16, 1), np.uint8)], axis=1)
    return (np.ascontiguousarray(c[:, e].reshape(128, -1)), np.ascontiguousarray(s[:, e]))
def join(*qs):
    return (np.concatenate([q[0] for q in qs], axis=1), np.concatenate([q[1] for q in qs], axis=1))
def put(q, e, v):
    c, s = q[0].reshape(128, -1, 4).copy(), q[1].copy(); c[:, e] = v[0].reshape(128, -1, 4); s[:, e] = v[1]
    return (c.reshape(128, -1), s)
def pk(c, s):
    return (np.ascontiguousarray(c), mx_ref.live(s))
def emit(q):
    return q[0], q[1]
def packed(v, rng):
    q = [mx_ref.quantize(np.ascontiguousarray(v[r])) for r in range(N)]
    return np.stack([a for a, b in q]), np.stack([mx_ref.plane(b, rng) for a, b in q])
def values_of_codes():
    e, c = np.zeros((128, 128, 4), np.float32), np.zeros((128, 2, 4), np.uint8)
    e[np.arange(128), np.arange(128), 0] = 1
    c[:127, :, 0] = np.arange(256).reshape(2, 128).T[:127]
    return mx_ref.matmul(mx_ref.quantize(e.reshape(128, 512).astype(BF)), (c.reshape(128, 8), np.full((16, 2), 127, np.uint8))).T.reshape(-1).astype(np.float64)
CODE_VALUE, SCALE_VALUE = values_of_codes(), 2.0 ** (np.arange(256) - 127.0)
def decode(q):
    return (CODE_VALUE[q[0]].reshape(16, 8, -1, 4) * SCALE_VALUE[q[1]][:, None, :, None] + 0.0).reshape(128, -1).astype(np.float32)
def f(rng, *shape):
    return mx_ref.flush((rng.standard_normal(shape, dtype=np.float32) * np.exp2(rng.integers(-2, 3, shape[:-1] + (1,)))).astype(BF))
def wide(rng, *shape, cols=0):
    v = rng.standard_normal(shape, dtype=np.float32) * np.exp2(rng.integers(-12, 13, shape)).astype(np.float32)
    if cols: v *= np.repeat(np.exp2(rng.integers(-cols, cols + 1, shape[:-2] + (1, shape[-1] // 4))) * (rng.random(shape[:-2] + (1, shape[-1] // 4)) > 0.0625), 4, axis=-1).astype(np.float32)
    return mx_ref.flush(v.astype(BF))
C = 352
STEP = [1, 2, 4]
def numbers_of(rng):
    return {"x": np.array(f(rng, N, 128, 4 * C)), "u": np.array(f(rng, N, 128, 512)), "v": np.array(f(rng, N, 128, 512))}
def stored(a, b):
    return {"lam": np.stack([gtable(a[r]) for r in range(N)]), "rho": np.stack([gtable(b[r]) for r in range(N)])}
def dealt(rng):
    e = np.tile(np.arange(C), (N, 8, 1))
    return np.stack([rng.permuted(e, axis=2), rng.permuted(e, axis=2)], axis=3).reshape(N, 8, 2 * C)
def lists(rng):
    a = dealt(rng)
    return stored(a, dealt(rng))
def layers(rng):
    return np.array(f(rng, N, 128, 2048)).reshape(N, 8, 16, 4, 8, 16, 4)
def weights(rng, w):
    c, p = packed(np.ascontiguousarray(w).reshape(N, 128, 2048), rng)
    return {"wc": c, "ws": p}
def unread(u):
    u = u.reshape(N, 128, 128, 4)
    u[:, :, ::16] = 0
    u[:, :, 1::16] = 0
    return u
def setup_inputs(rng):
    return {**numbers_of(rng), **lists(rng), **weights(rng, layers(rng))}
def setup_inputs_ties(rng):
    d = numbers_of(rng)
    o = rng.permutation(N)
    s = rng.integers(-1, 2, (N, 8, 2, C)).astype(np.float32)
    s[o[1]] = 1
    s[o[2]] = -1
    x = d["x"].reshape(N, 8, 16, C, 4)
    x[:, :, :2] = 0
    x[:, :, :2, :, 0] = s.astype(BF)
    c = np.ones(N, np.float32)
    c[o[0]] = 0
    u = unread(d["u"])
    for h in range(0, 128, 16):
        for i in range(2): u[:, h + i, h + i, 0] = c.astype(BF)
    w = layers(rng)
    w[:, :, :, :, :, :8] = 0
    for g in range(8): w[:, g, 15, 0, g, 15, 0] = 2.0 ** 8
    return {"x": x.reshape(N, 128, 4 * C), "u": u.reshape(N, 128, 512), "v": d["v"], **lists(rng), **weights(rng, w)}
def setup_inputs_near(rng):
    d = numbers_of(rng)
    lo = np.unique(np.minimum(np.arange(N), np.arange(N) ^ STEP[0]))
    o = np.zeros(N, np.int64)
    o[lo] = rng.permutation(N // 2) % 2
    o[lo ^ STEP[0]] = o[lo]
    k = np.where(o == 0, 2.0 ** -30, 1.0).astype(np.float32)
    some = rng.permutation(8)[:4]
    x = d["x"].astype(np.float32).reshape(N, 8, 16, C, 4)
    x[:, :, :8] = 0
    x[:, some, 8:] = 0
    for g in some: x[:, g, 15, :, 0] = k[:, None]
    for i in range(2):
        s = rng.integers(-1, 2, (N, 8, C)) * k[:, None, None]
        x[:, :, 2 * i, :, 0] = 1.125 * s
        x[:, :, 2 * i + 1, :, 0] = -1.25 * s
        x[:, :, 6, :, i] = rng.choice([-1.0, 1.0], (N, 8, C)) * k[:, None, None]
        x[:, :, 6, :, 2 + i] = rng.choice([-1.0, 1.0], (N, 8, C)) * k[:, None, None]
    x[:, :, 7, :, 0] = k[:, None, None]
    for r in range(N):
        for g in rng.permutation(8)[:4]: x[r, g, 2 * rng.integers(2), rng.integers(C), 0] = 2.0 ** 30 * rng.choice([-1.0, 1.0])
    u = unread(d["u"])
    for h in range(0, 128, 16):
        for i in range(2):
            u[:, h + 2 * i, h + i, 0] = (1.125 * k).astype(BF)
            u[:, h + 2 * i + 1, h + i, 0] = k.astype(BF)
            u[:, h + 4 + i, h + i, 0] = k.astype(BF)
    w = layers(rng)
    w[:, :, :8] = 0
    w[:, :, :, :, :, :8] = 0
    w[:, :8] = 0
    for g in range(8):
        for i in range(2): w[:, g, 6, 0, g, 4 + i, i] = 2.0 ** -8
        w[:, g, 7, 0, g, 7, 0] = 32.0
    for g in some:
        for i in range(2):
            u[:, 16 * g + 8 + 2 * i, 16 * g + i, 0] = (1.125 * k).astype(BF)
            u[:, 16 * g + 9 + 2 * i, 16 * g + i, 0] = k.astype(BF)
            w[:, g, 6, 0, g, 8 + 2 * i, 2 + i] = 1.125 * 2.0 ** -8
            w[:, g, 6, 0, g, 9 + 2 * i, 2 + i] = -1.25 * 2.0 ** -8
        w[:, g, 7, 0, g, 14, 0] = 32.0
    return {"x": x.reshape(N, 128, 4 * C).astype(BF), "u": u.reshape(N, 128, 512), "v": d["v"], **lists(rng), **weights(rng, w)}
def setup_inputs_odd(rng):
    d = numbers_of(rng)
    x = d["x"].astype(np.float32).reshape(N, 8, 16, C, 4)
    x[:, :, 8:] = 0
    x[:, :, 0, :, 0] = 1.96875 * 2.0 ** 8
    for i in range(2):
        x[:, :, 1 + 2 * i, :, 0] = 2.0 ** -5
        x[:, :, 2 + 2 * i, :, 0] = (7 + 2 * rng.integers(0, 2, (N, 8, C))) * 2.0 ** -8
    x[:, :, 8, :, 0] = -1.125
    x[:, :, 10, :, 0] = 0.0703125 * rng.choice([-1.0, 1.0], (N, 8, C))
    u = unread(d["u"])
    for h in range(0, 128, 16):
        for i in range(2):
            c = rng.choice([-1.0, 1.0], N).astype(np.float32)
            u[:, h + 1 + 2 * i, h + i, 0] = c.astype(BF)
            u[:, h + 2 + 2 * i, h + i, 0] = (-1.125 * c).astype(BF)
    w = np.zeros((N, 8, 16, 4, 8, 16, 4), np.float32)
    for g in range(8):
        w[:, g, 8, 0, g, 8, 0] = -28.0
        w[:, g, 2, 0, g, 12, 0] = 32.0
        for b in range(4): w[:, g, 10, b, g, 9, 0] = -2.0 ** (b - 5)
    return {"x": x.reshape(N, 128, 4 * C).astype(BF), "u": u.reshape(N, 128, 512), "v": d["v"], **lists(rng), **weights(rng, w.astype(BF))}
def setup_inputs_ends(rng):
    d = numbers_of(rng)
    o, e = rng.permutation(N) % 4, rng.permutation(N) % 4
    s = rng.choice([-1.0, 1.0], (N, 128, C, 4))
    s[o == 0] = -1
    s[o == 1] = rng.choice([-1.0, 1.0], (N, 1, C, 1))[o == 1]
    x = s * (0.93 + 0.02 * rng.random((N, 128, C, 4))) * 2.0 ** 30
    x[o == 3] = 2.0 ** -30
    size = np.where(o == 3, 2.0 ** -30, 2.0 ** 30)
    u = unread(d["u"])
    for r in range(N):
        h = rng.permutation(8)
        for i in range(2):
            c = np.where(h < 2, 0.0, ((h >> i) % 2) * 2.0 - 1.0) * size[r]
            u[r, :, i::16] = c.astype(np.float32).astype(BF)[None, :, None]
    v = rng.choice([-1.0, 1.0], (N, 128, 512)) * np.where(o < 2, 2.0 ** 30, 2.0 ** -30)[:, None, None]
    t = rng.integers(0, C, (2, N, 8, 2 * C))
    t[:, e == 0] = C - 1
    t[:, e == 1] = 0
    t[:, e == 2] = np.arange(2 * C) % 2 * (C - 1)
    w = np.zeros((N, 128, 4, 128, 4), np.float32)
    j = np.arange(127)
    for b in range(4): w[:, j, b, j, b] = np.array([-0.25, -0.25, -2.0 ** -8, 32.0])[o][:, None]
    return {"x": x.astype(np.float32).reshape(N, 128, 4 * C).astype(BF), "u": u.reshape(N, 128, 512), "v": v.astype(np.float32).astype(BF), **stored(t[0], t[1]), **weights(rng, w.astype(BF))}
def setup_inputs_spread(rng):
    d = setup_inputs(rng)
    d["x"] = wide(rng, N, 128, 4 * C, cols=6)
    return d
def check_inputs(d):
    b = []
    for k in ("x", "u", "v"):
        a = np.abs(d[k].astype(np.float32))
        if not (np.isfinite(a).all() and ((a == 0) | (a >= 2.0 ** -30) & (a <= 2.0 ** 30)).all()): b.append("a value of " + k)
    for k in ("lam", "rho"):
        if not ((d[k] >= 0) & (d[k] < C)).all(): b.append("an entry of " + k)
    none, least, most = [emit(mx_ref.quantize(np.full((128, 16), k, np.float32).astype(BF)))[1][0, 0] for k in (0.0, 2.0 ** -8, 2.0 ** 8)]
    for r in range(N):
        if ((d["wc"][r] == 0x7F) | (d["wc"][r] == 0xFF)).any(): b.append("wc: a code that is no number")
        s = mx_ref.live(d["ws"][r])
        if ((s != none) & ((s < least) | (s > most))).any(): b.append("ws: a scale out of range")
        if (((d["wc"][r].reshape(16, 8, 512, 4) & 0x7F) != 0) & (s == none)[:, None, :, None]).any(): b.append("wc: a code other than zero under the scale of zeros")
    return b
def swapped(t, where):
    a = t.reshape(8, C, 2)
    return np.where(where[:, :, None], a[:, :, ::-1], a).reshape(8, 2 * C)
def reference(x, u, v, lam, rho, wc, ws):
    qu = [mx_ref.quantize(u[r]) for r in range(N)]
    lay = [pk(wc[r], ws[r]) for r in range(N)]
    left, right = [gentries(lam[r]) for r in range(N)], [gentries(rho[r]) for r in range(N)]
    now = [x[r] for r in range(N)]
    q = [mx_ref.quantize(now[r]) for r in range(N)]
    s = [mx_ref.matmul(qu[r], q[r]) for r in range(N)]
    for step in STEP:
        at, mid, sent = [], [], []
        for r in range(N):
            bit = (s[r][::16] > 0).astype(np.int64)
            up, down = np.zeros((8, C), np.int64), np.zeros((8, C), np.int64)
            up[0] = np.arange(C)
            down[7] = np.arange(C)
            for g in range(7):
                up[g + 1] = left[r][g][2 * up[g] + bit[g]]
            for g in range(7, 0, -1):
                down[g - 1] = right[r][g][2 * down[g] + bit[g]]
            at.append(np.take_along_axis(up, down, axis=1))
            mid.append(((now[r].astype(np.float32) + gcols(now[r], at[r]).astype(np.float32)) * np.float32(0.5)).astype(BF))
            z = mx_ref.quantize(mid[r])
            sent.append(mx_ref.quantize(tile([mx_ref.matmul(pick(lay[r], np.arange(128 * b, 128 * b + 128)), z) * np.float32(0.03125) for b in range(4)])))
        for r in range(N):
            p = r ^ step
            far = gcols(decode(sent[p]).astype(BF), np.take_along_axis(at[p], at[r], axis=1))
            now[r] = (mid[r].astype(np.float32) + far.astype(np.float32)).astype(BF)
            q[r] = mx_ref.quantize(now[r])
            s[r] = mx_ref.matmul(qu[r], q[r])
            left[r], right[r] = swapped(left[r], s[r][1::16] < 0), swapped(right[r], s[r][1::16] > 0)
    y, lr = np.zeros((N, 128, C), np.float32), np.zeros((N, 8, 4 * C), np.float32)
    oc, osc = np.zeros((N, 128, 4 * C), np.uint8), np.zeros((N, 16, C), np.uint8)
    for r in range(N):
        y[r] = mx_ref.matmul(mx_ref.quantize(v[r]), q[r])
        lr[r] = np.concatenate([left[r], right[r]], axis=1)
        oc[r], osc[r] = emit(q[r])
    return {"y": y, "lr": lr, "oc": oc, "osc": osc}

@@ -1,0 +1,337 @@
+from concourse.bass import DstId, RemoteDMATransfer
+from concourse.mybir import dt, AluOpType, ActivationFunctionType
+
+C = 352
+STEP = (1, 2, 4)
+CH = ((0, 192), (192, 352))
+A = AluOpType
+COPY = ActivationFunctionType.Copy
+SIGN = ActivationFunctionType.Sign
+F8 = "float8_e4m3fn_x4"
+
+SCRATCH = {
+    "xt": ("sbuf", [128, 4 * C], "bfloat16"), "xh": ("sbuf", [128, 4 * C], "bfloat16"),
+    "vt": ("sbuf", [128, 4 * C], "bfloat16"), "hp": ("sbuf", [128, 4 * C], "bfloat16"),
+    "hl": ("sbuf", [128, 4 * C], "bfloat16"), "dp": ("sbuf", [128, 4 * C], "bfloat16"),
+    "ut": ("sbuf", [128, 512], "bfloat16"), "vv": ("sbuf", [128, 512], "bfloat16"), "et": ("sbuf", [128, 2048], "bfloat16"),
+    "one": ("sbuf", [128, 512], "bfloat16"), "xi": ("sbuf", [128, 4 * C], "bfloat16"),
+    "xq": ("sbuf", [128, C], F8), "xs": ("sbuf", [128, C], "uint8"),
+    "vq": ("sbuf", [128, C], F8), "vs": ("sbuf", [128, C], "uint8"),
+    "uq": ("sbuf", [128, 128], F8), "us": ("sbuf", [128, 128], "uint8"),
+    "pq": ("sbuf", [128, 256], F8), "ps": ("sbuf", [128, 256], "uint8"),
+    "zq": ("sbuf", [128, 128], F8), "zs": ("sbuf", [128, 128], "uint8"),
+    "eq": ("sbuf", [128, 512], F8), "es": ("sbuf", [128, 512], "uint8"),
+    "wq": ("sbuf", [128, 512], F8), "wp": ("sbuf", [128, 512], "uint8"),
+    "ti": ("sbuf", [128, 704], "int32"), "tf": ("sbuf", [128, 704], "float32"), "idt": ("sbuf", [128, 704], "int32"),
+    "d0": ("sbuf", [128, 1056], "float32"), "d1": ("sbuf", [128, 1056], "float32"), "tw": ("sbuf", [128, 1056], "float32"),
+    "sb": ("sbuf", [128, C], "float32"), "bra": ("sbuf", [128, 128], "float32"), "brb": ("sbuf", [128, 128], "float32"),
+    "gm": ("sbuf", [128, 128], "float32"), "g0": ("sbuf", [128, 128], "float32"), "g2": ("sbuf", [128, 128], "float32"),
+    "g4": ("sbuf", [128, 128], "float32"), "g6": ("sbuf", [128, 128], "float32"), "zt": ("sbuf", [128, 128], "float32"),
+    "off": ("sbuf", [128, 8], "uint16"), "sl": ("sbuf", [128, 16], "uint16"), "ul": ("sbuf", [128, 16], "uint16"),
+    "lw": ("sbuf", [128, 768], "float32"), "rl": ("sbuf", [128, 32], "float32"), "ri": ("sbuf", [128, 32], "int32"),
+    "ro": ("sbuf", [128, 22], "uint16"), "gcm": ("sbuf", [128, C], "float32"), "zc": ("sbuf", [128, C], "float32"),
+    "ki": ("sbuf", [128, 22], "int32"), "ko": ("sbuf", [128, 22], "uint16"),
+    "ci": ("sbuf", [128, 16], "int32"), "cf": ("sbuf", [128, 16], "float32"), "fw": ("sbuf", [128, 16], "float32"),
+    "fc": ("sbuf", [128, 128], "float32"), "c3": ("sbuf", [128, 128], "float32"), "z8": ("sbuf", [128, 8], "float32"),
+    "yt": ("sbuf", [128, C], "float32"), "lt": ("sbuf", [128, 704], "float32"),
+    "pm": ("psum", [128, 4096], "float32"),
+}
+for _r in range(3):
+    SCRATCH["hq%d" % _r] = ("sbuf", [128, C], F8)
+    SCRATCH["hs%d" % _r] = ("sbuf", [128, C], "uint8")
+    SCRATCH["aq%d" % _r] = ("sbuf", [128, C], F8)
+    SCRATCH["as%d" % _r] = ("sbuf", [128, C], "uint8")
+SEMAPHORES = (["sv", "ss", "st", "sg", "lu", "lx", "lt", "lid", "lw", "lv", "snt", "outs"]
+              + ["hop%d" % r for r in range(3)] + ["arr%d%d" % (r, c) for r in range(3) for c in range(2)])
+
+
+def rank_program(g, core, T, topo):
+    rank = T.rank_of(core)
+    if rank is None:
+        return
+    Q = {"v": g.vector, "s": g.scalar, "t": g.tensor, "g": g, "y": g.sync}
+    SEM = {"v": "sv", "s": "ss", "t": "st", "g": "sg"}
+    total = {}
+    waited = {}
+    gens = {}
+
+    def need(qn, toks):
+        best = {}
+        for s, n in toks:
+            n = total[s] if n is None else n
+            best[s] = max(best.get(s, 0), n)
+        for s, n in best.items():
+            if waited.get((qn, s), 0) < n:
+                Q[qn].wait_ge(T.sem[s], n)
+                waited[(qn, s)] = n
+
+    def before(qn, R, W):
+        toks = []
+        for k in R:
+            toks += gens.setdefault(k, [[], [], []])[1]
+        for k in W:
+            e = gens.setdefault(k, [[], [], []])
+            if e[2]:
+                gens[k] = e = [e[1] + e[2], [], []]
+            toks += e[0]
+        need(qn, toks)
+
+    def after(tok, R, W):
+        for k in R:
+            gens[k][2].append(tok)
+        for k in W:
+            gens[k][1].append(tok)
+
+    def op(qn, fn, args, R, W, kw=None):
+        before(qn, R, W)
+        s = SEM[qn]
+        fn(*args, **(kw or {})).then_inc(T.sem[s], 1)
+        total[s] = total.get(s, 0) + 1
+        after((s, total[s]), R, W)
+
+    def dma(qn, out, in_, R, W, sem):
+        before(qn, R, W)
+        Q[qn].dma_start(out, in_).then_inc(T.sem[sem], 16)
+        total[sem] = total.get(sem, 0) + 16
+        after((sem, None), R, W)
+
+    V, S, TE = g.vector, g.scalar, g.tensor
+
+    def ts(out, in0, s1, s2, o0, o1, R, W):
+        if o1 is None:
+            op("v", V.tensor_scalar, (out, in0, s1, None, o0), R, W)
+        else:
+            op("v", V.tensor_scalar, (out, in0, s1, s2, o0, o1), R, W)
+
+    def tt(out, a, b, o, R, W):
+        op("v", V.tensor_tensor, (out, a, b, o), R, W)
+
+    def tc(out, a, R, W):
+        op("v", V.tensor_copy, (out, a), R, W)
+
+    def act(out, a, R, W, **kw):
+        op("s", S.activation, (out, a, COPY), R, W, kw)
+
+    def bank(i, n=C):
+        return T.pm[:, 512 * i:512 * i + n]
+
+    def mm(i, n, lq, ls, rq, rs, R):
+        op("t", TE.matmul_mx, (bank(i, n), lq, ls, rq, rs, True, True), R, ["b%d" % i])
+
+    def quant(q, s, t, R, W):
+        op("v", V.quantize_mx, (q, s, t), R, W)
+
+    def u8(v):
+        return v.bitcast(dt.uint8)
+
+    dma("s", T.ut[:], T.u[:], [], ["ut"], "lu")
+    dma("y", T.xt[:], T.x[:], [], ["xt"], "lx")
+    for h in range(8):
+        qn = "y" if h % 2 else "s"
+        if h == 1:
+            dma(qn, T.ti[16:23, :], T.lam[0:112, :], [], ["ti"], "lt")
+            dma(qn, T.ti[23:24, :], T.rho[0:16, :], [], ["ti"], "lt")
+        else:
+            dma(qn, T.ti[16 * h:16 * h + 8, :], T.lam[:], [], ["ti"], "lt")
+        dma(qn, T.ti[16 * h + 9:16 * h + 16, :], T.rho[16:128, :], [], ["ti"], "lt")
+    dma("s", u8(T.wq[:, :]), T.wc[:], [], ["wq"], "lw")
+    dma("s", T.wp[:], T.ws[:], [], ["wq"], "lw")
+    dma("s", T.vv[:], T.v[:], [], ["vv"], "lv")
+
+    def iota(out, pat, base, cm, W, f=True):
+        kw = {"allow_small_or_imprecise_dtypes": True} if f else {}
+        op("g", g.iota, (out, pat, base, cm), [], W, kw)
+    iota(T.ci[:, 0:1], [[0, 1]], 0, 1, ["ci0"], False)
+    iota(T.fw[:, 0:4], [[16, 4]], 0, 0, ["fw"])
+    iota(T.fw[:, 4:8], [[1, 4]], 0, 0, ["fw"])
+    iota(T.fw[:, 8:12], [[32, 2], [48, 2]], 0, 0, ["fw"])
+    iota(T.fw[:, 12:16], [[2, 2], [4, 2]], 0, 0, ["fw"])
+    iota(T.fc[:, 0:64], [[32, 2], [48, 2], [1, 16]], 0, 0, ["fc"])
+    iota(T.fc[:, 64:128], [[2, 2], [4, 2], [32, 16]], 0, 0, ["fc"])
+    iota(T.idt[:, :], [[1, 8], [0, 2], [8, 44]], 0, 0, ["idt"], False)
+    dma("y", T.ti[8:128:16, :], T.idt[0:8, :], ["idt"], ["ti"], "lt")
+    op("v", V.memset, (T.z8[:], 0.0), [], ["z8"])
+
+    def I(k):
+        return T.ci[:, k:k + 1]
+
+    def F(k):
+        return T.cf[:, k:k + 1]
+    SR, AND = A.logical_shift_right, A.bitwise_and
+    ts(I(1), I(0), 15, None, AND, None, ["ci0"], ["ci1"])
+    ts(I(2), I(0), 3, 1, SR, AND, ["ci0"], ["ci2"])
+    ts(I(3), I(0), 7, None, AND, None, ["ci0"], ["ci3"])
+    ts(I(4), I(0), 4, None, SR, None, ["ci0"], ["ci4"])
+    ts(I(5), I(0), 5, None, SR, None, ["ci0"], ["ci5"])
+    ts(I(6), I(0), 4, 1, SR, AND, ["ci0"], ["ci6"])
+    ts(I(7), I(2), -2, 1, A.mult, A.add, ["ci2"], ["ci7"])
+    tt(I(8), I(7), I(1), A.add, ["ci7", "ci1"], ["ci8"])
+    ts(I(9), I(8), 7, None, AND, None, ["ci8"], ["ci9"])
+    ts(F(0), I(9), 16.0, None, A.mult, None, ["ci9"], ["f0"])
+    ts(F(1), I(3), 16.0, 1.0, A.mult, A.add, ["ci3"], ["f1"])
+    ts(F(2), I(1), 7.0, -112.0, A.is_equal, A.mult, ["ci1"], ["f2"])
+    ts(T.ul[:, 0:8], T.z8[:], F(0), None, A.add, None, ["z8", "f0"], ["ul"])
+    ts(T.ul[:, 8:16], T.z8[:], F(1), None, A.add, None, ["z8", "f1"], ["ul"])
+    need("v", [("sv", total["sv"])])
+    ts(T.ul[:, 9:10], F(2), F(1), None, A.add, None, ["f1", "f2"], ["ul"])
+    ts(F(3), I(7), 1.0, None, A.mult, None, ["ci7"], ["f3"])
+    ts(F(4), I(0), 23.0, -2.0, A.is_equal, A.mult, ["ci0"], ["f4"])
+    tt(F(5), F(3), F(4), A.add, ["f3", "f4"], ["f5"])
+    tc(F(6), I(1), ["ci1"], ["f6"])
+    ts(F(7), I(1), 32.0, None, A.mult, None, ["ci1"], ["f7"])
+    tc(F(8), I(6), ["ci6"], ["f8"])
+    ts(F(9), I(4), 48.0, F(6), A.mult, A.add, ["ci4", "f6"], ["f9"])
+    ts(F(10), I(4), 4.0, F(7), A.mult, A.add, ["ci4", "f7"], ["f10"])
+    ts(F(11), I(6), 16.0, None, A.mult, None, ["ci6"], ["f11"])
+    ts(F(12), I(5), 96.0, F(11), A.mult, A.add, ["ci5", "f11"], ["f12"])
+    ts(F(13), I(5), 8.0, F(8), A.mult, A.add, ["ci5", "f8"], ["f13"])
+    tt(F(14), F(12), F(6), A.add, ["f12", "f6"], ["f14"])
+    tt(F(15), F(13), F(7), A.add, ["f13", "f7"], ["f15"])
+    for k, f in ((0, 9), (4, 10), (8, 14), (12, 15)):
+        ts(T.sl[:, k:k + 4], T.fw[:, k:k + 4], F(f), 351.0, A.add, A.min, ["fw", "f%d" % f], ["sl"])
+    ts(T.fc[:, 0:64], T.fc[:, 0:64], F(12), 351.0, A.add, A.min, ["fc", "f12"], ["fca"])
+    ts(T.fc[:, 64:128], T.fc[:, 64:128], F(13), 351.0, A.add, A.min, ["fc", "f13"], ["fca"])
+    ts(T.c3[:], T.fc[:], 3.0, None, A.mult, None, ["fca"], ["c3"])
+    op("v", V.memset, (T.one[:], 1.0), [], ["one"])
+    op("v", V.memset, (T.lw[:], 0.0), [], ["lwz"])
+    for k, val in ((0, 0), (1, 1), (2, -1)):
+        iota(T.d0[:, k:1056:3], [[0, C]], val, 0, ["phi" if k == 1 else "d0c"])
+    quant(T.uq[:], T.us[:], T.ut[:], ["ut"], ["uq"])
+    op("v", V.tensor_copy, (T.pq[:, 0:256].bitcast(dt.uint32), T.uq[:, 0:128].bitcast(dt.uint32).indirect(T.ul[:, 0:16])), ["uq", "ul"], ["pq"])
+    act(T.ps[:, 0:256], T.us[:, 0:128].indirect(T.ul[:, 0:16]), ["uq", "ul"], ["pq"])
+    quant(T.xq[:], T.xs[:], T.xt[:], ["xt"], ["xq"])
+
+    def scores(rows):
+        for k in rows:
+            mm(k, C, T.pq[:, 128 * k:128 * k + 128], T.ps[:, 128 * k:128 * k + 128], T.xq[:], T.xs[:], ["pq", "xq"])
+    scores([0])
+    for r in range(8):
+        e, o = T.ti[:, 88 * r:88 * r + 44], T.ti[:, 88 * r + 44:88 * r + 88]
+        tt(T.d1[:, 3 * r + 1:1056:24], o, e, A.add, ["ti"], ["d1s"])
+    for r in range(8):
+        e, o = T.ti[:, 88 * r:88 * r + 44], T.ti[:, 88 * r + 44:88 * r + 88]
+        tt(T.d1[:, 3 * r:1056:24], o, e, A.subtract, ["ti"], ["d1d"])
+    act(T.d1[:, 2:1056:3], T.d1[:, 1:1056:3], ["d1s"], ["d1n"], scale=3.0)
+    act(T.d1[:, 1:1056:3], T.d1[:, 1:1056:3], ["d1s"], ["d1m"], scale=1.5)
+    act(T.d1[:, 0:1056:3], T.d1[:, 0:1056:3], ["d1d"], ["d1b"], scale=1.5)
+    iota(T.rl[:, :], [[0, 2], [96, 16]], -287, 3, ["rli"])
+    before("g", ["lwz"], [])
+    iota(T.lw[0:32, 0:384], [[3, 384]], 1, 0, ["lw"])
+    for b in range(4):
+        op("g", g.affine_select, (T.et[:, 512 * b:512 * b + 512], T.one[:], [[-1, 512]], A.is_equal, 0.0, b, 4), ["one"], ["et"])
+
+    K12 = (T.ko[:, 0:12], T.ko[:, 12:22])
+
+    def plane(t, b, c0=0, c1=C):
+        return t[:, C * b + c0:C * b + c1]
+
+    def inter(t, b, c0=0, c1=C):
+        return t[:, 4 * c0 + b:4 * c1:4]
+
+    for rnd in range(3):
+        partner = T.cores[rank ^ STEP[rnd]]
+        if rnd:
+            op("s", S.activation, (T.d0[:, 1:1056:3], bank(1), SIGN), ["b1", "f5"], ["phi"], {"bias": 2.0 ** -94, "scale": F(5)})
+        for b in range(4):
+            act(plane(T.xh, b), inter(T.xt, b), ["xt"], ["xh%d" % b], scale=0.5)
+        act(T.xi[:], T.xt[:], ["xt"], ["xi"], scale=0.5)
+        ts(T.sb[:], bank(0), 0.0, 1.0, A.is_le, A.add, ["b0"], ["sb"])
+        tt(T.gm[:], T.sb[:].indirect(T.sl[:, 8:16]), T.c3[:], A.add, ["sb", "sl", "c3"], ["gm"])
+
+        def wrap(src, key, ql, qr):
+            op("v", V.transpose, (T.zt[:], src), [key], ["zt"])
+            tc(T.off[:, 0:4], T.zt[:, ql:64:16], ["zt"], ["off"])
+            tc(T.off[:, 4:8], T.zt[:, 64 + qr:128:16], ["zt"], ["off"])
+        wrap(T.gm[:], "gm", 7, 8)
+        tc(T.bra[:], T.sb[:].indirect(T.sl[:, 0:8]), ["sb", "sl"], ["bra"])
+        op("v", V.tensor_tensor_scan, (T.tw[:], T.d0[:], T.d1[:], 0.0, A.mult, A.add), ["d0c", "phi", "d1b", "d1m", "d1n"], ["tw"])
+        tc(T.brb[:], T.sb[:].indirect(T.sl[:, 8:16]), ["sb", "sl"], ["brb"])
+        hop = "hop%d" % rnd
+
+        def land(qn, gt, key, lists):
+            for kind, q, to in lists:
+                a, h = to // 2, to % 2
+                if kind == "l":
+                    for d in (0, 16):
+                        dma(qn[0], T.lw[32 * a + d:32 * a + d + 1, 384 * h:384 * h + 384], gt[q:128:16, 0:48], [key, "lwz"], ["lw"], hop)
+                        qn = qn[1:] + qn[:1]
+                else:
+                    dma(qn[0], T.rl[32 * a:32 * a + 32, 16 * h:16 * h + 16], gt[q:128:16, 64:128], [key, "rli"], ["rl"], hop)
+                    qn = qn[1:] + qn[:1]
+        for t in range(7):
+            name = "gm" if t % 2 else "g%d" % t
+            tt(T[name][:], T.tw[:].indirect(T.off[:, 0:8]), (T.brb if t % 2 else T.bra)[:], A.add, ["tw", "off", "brb" if t % 2 else "bra"], [name])
+            if t < 6:
+                wrap(T[name][:], name, t, 15 - t)
+            if t % 2 == 0:
+                todo = [("l", t, t + 1), ("r", 15 - t, 6 - t)]
+                if t:
+                    todo += [("l", 8, t), ("r", 8, 7 - t)]
+                land("y" if t < 6 else "ys", T[name], name, todo)
+        ts(T.ri[:], T.rl[:], -1.5, 1.0 / 3.0, A.add, A.mult, ["rl", "rli"], ["ri"])
+        for h in range(2):
+            ts(T.ro[:, h:22:2], T.ri[:, 16 * h:16 * h + 11], 384.0 * h, None, A.add, None, ["ri"], ["ro"])
+        tc(T.gcm[:], T.lw[:].indirect(T.ro[:]), ["lw", "ro"], ["gcm"])
+        op("v", V.transpose, (T.zc[:], T.gcm[:]), ["gcm"], ["zc"])
+        ts(T.ki[:], T.zc[:, 0:352:16], -1.5, 1.0 / 3.0, A.add, A.mult, ["zc"], ["ki"])
+        tc(T.ko[:], T.ki[:], ["ki"], ["ko"])
+        for c, (c0, c1) in enumerate(CH):
+            for b in range(4):
+                tt(inter(T.vt, b, c0, c1), plane(T.xh, b).indirect(K12[c]), inter(T.xi, b, c0, c1), A.add, ["xh%d" % b, "xi", "ko"], ["vt%d" % c])
+            quant(T.vq[:, c0:c1], T.vs[:, c0:c1], T.vt[:, 4 * c0:4 * c1], ["vt%d" % c], ["vq%d" % c])
+            for b in range(4):
+                mm(4 * c + b, c1 - c0, T.wq[:, 128 * b:128 * b + 128], T.wp[:, 128 * b:128 * b + 128], T.vq[:, c0:c1], T.vs[:, c0:c1], ["wq", "vq%d" % c])
+                if c == 0 or b % 2:
+                    act(plane(T.hp, b, c0, c1), bank(4 * c + b, c1 - c0), ["b%d" % (4 * c + b)], ["hp%d" % b], scale=0.03125)
+            if c == 1:
+                for b in (0, 2):
+                    ts(plane(T.hp, b, c0, c1), bank(4 + b, c1 - c0), 0.03125, None, A.mult, None, ["b%d" % (4 + b)], ["hp%d" % b])
+        hq, hs, aq, as_ = T["hq%d" % rnd], T["hs%d" % rnd], T["aq%d" % rnd], T["as%d" % rnd]
+        rid, pid = topo.addr(partner)[0:2]
+        mask = topo.mask(core, partner)
+        ne = len(topo.engines(core, partner))
+        for c, (c0, c1) in enumerate(CH):
+            for b in (1, 3):
+                act(inter(T.hl, b, c0, c1), plane(T.hp, b).indirect(K12[c]), ["hp%d" % b, "ko"], ["hl%d" % c])
+            for b in (0, 2):
+                tc(inter(T.hl, b, c0, c1), plane(T.hp, b).indirect(K12[c]), ["hp%d" % b, "ko"], ["hl%d" % c])
+            quant(hq[:, c0:c1], hs[:, c0:c1], T.hl[:, 4 * c0:4 * c1], ["hl%d" % c], ["hq%d%d" % (rnd, c)])
+            before("g", ["hq%d%d" % (rnd, c)], [])
+            arr = T.sem["arr%d%d" % (rnd, c)]
+            g.remote_dma(u8(aq[:, c0:c1]), u8(hq[:, c0:c1]), arr, T.sem.snt, pid, rid, mask)
+            g.remote_dma(as_[:, c0:c1], hs[:, c0:c1], arr, T.sem.snt, pid, rid, mask)
+            total["snt"] = total.get("snt", 0) + 2 * ne
+            total["arr%d%d" % (rnd, c)] = 2 * ne
+        if rnd:
+            tt(T.d1[:, 0:1056:3], T.d1[:, 0:1056:3], T.d0[:, 1:1056:3], A.mult, ["d1b", "phi"], ["d1b"])
+        else:
+            quant(T.eq[:], T.es[:], T.et[:], ["et"], ["eq"])
+        if rnd == 2:
+            quant(T.zq[:], T.zs[:], T.vv[:], ["vv"], ["zq"])
+        for c, (c0, c1) in enumerate(CH):
+            need("t", [("arr%d%d" % (rnd, c), None)])
+            for b in range(4):
+                mm(4 * c + b, c1 - c0, T.eq[:, 128 * b:128 * b + 128], T.es[:, 128 * b:128 * b + 128], aq[:, c0:c1], as_[:, c0:c1], ["eq"])
+                if c == 0 or b % 2:
+                    act(plane(T.dp, b, c0, c1), bank(4 * c + b, c1 - c0), ["b%d" % (4 * c + b)], ["dp%d" % b])
+                else:
+                    tc(plane(T.dp, b, c0, c1), bank(4 * c + b, c1 - c0), ["b%d" % (4 * c + b)], ["dp%d" % b])
+        for b in (0, 2, 1, 3):
+            tt(inter(T.xt, b), plane(T.dp, b).indirect(T.ko[:]), inter(T.vt, b), A.add, ["dp%d" % b, "ko", "vt0", "vt1"], ["xt"])
+        quant(T.xq[:], T.xs[:], T.xt[:], ["xt"], ["xq"])
+        scores([0, 1] if rnd < 2 else [1])
+
+    mm(2, C, T.zq[:], T.zs[:], T.xq[:], T.xs[:], ["zq", "xq"])
+    dma("y", T.oc[:], u8(T.xq[:, :]), ["xq"], [], "outs")
+    for k in range(4):
+        dma("y", T.osc[4 * k:4 * k + 4, :], T.xs[32 * k:32 * k + 4, :], ["xq"], [], "outs")
+    op("s", S.activation, (T.d0[:, 1:1056:3], bank(1), SIGN), ["b1", "f5"], ["phi"], {"bias": 2.0 ** -94, "scale": F(5)})
+    tc(T.yt[:], bank(2), ["b2"], ["yt"])
+    dma("y", T.y[:], T.yt[:], ["yt"], [], "outs")
+    op("v", V.tensor_tensor_scan, (T.tw[:], T.d0[:], T.d1[:], 0.0, A.mult, A.add), ["d0c", "phi", "d1b", "d1m", "d1n"], ["tw"])
+    ts(T.lt[:, 0:704:2], T.tw[:, 2:1056:3], 1.0 / 3.0, None, A.mult, None, ["tw"], ["lt"])
+    act(T.lt[:, 1:704:2], T.tw[:, 1:1056:3], ["tw"], ["lt"], scale=1.0 / 3.0)
+    dma("y", T.lr[0:8, 0:704], T.lt[0:8, :], ["lt"], [], "outs")
+    dma("s", T.lr[1:8, 704:1408], T.lt[9:16, :], ["lt"], [], "outs")
+    dma("s", T.lr[0:1, 704:1408], T.lt[23:24, :], ["lt"], [], "outs")
+    need("g", [(s, None) for s in total if not s.startswith("arr")])

@@ -4,6 +4,8 @@ from concourse.mybir import dt, AluOpType, ActivationFunctionType
 C = 352
 STEP = (1, 2, 4)
 CH = ((0, 192), (192, 352))
+PLACES = 1
+LATE = 3
 A = AluOpType
 COPY = ActivationFunctionType.Copy
 SIGN = ActivationFunctionType.Sign
@@ -25,12 +27,14 @@ SCRATCH = {
     "ti": ("sbuf", [128, 704], "int32"), "tf": ("sbuf", [128, 704], "float32"), "idt": ("sbuf", [128, 704], "int32"),
     "d0": ("sbuf", [128, 1056], "float32"), "d1": ("sbuf", [128, 1056], "float32"), "tw": ("sbuf", [128, 1056], "float32"),
     "sb": ("sbuf", [128, C], "float32"), "bra": ("sbuf", [128, 128], "float32"), "brb": ("sbuf", [128, 128], "float32"),
-    "gm": ("sbuf", [128, 128], "float32"), "g0": ("sbuf", [128, 128], "float32"), "g2": ("sbuf", [128, 128], "float32"),
+    "gm": ("sbuf", [128, 128], "float16"), "zm": ("sbuf", [128, 128], "float16"), "g0": ("sbuf", [128, 128], "float32"), "g2": ("sbuf", [128, 128], "float32"),
     "g4": ("sbuf", [128, 128], "float32"), "g6": ("sbuf", [128, 128], "float32"), "zt": ("sbuf", [128, 128], "float32"),
     "off": ("sbuf", [128, 8], "uint16"), "sl": ("sbuf", [128, 16], "uint16"), "ul": ("sbuf", [128, 16], "uint16"),
     "lw": ("sbuf", [128, 768], "float32"), "rl": ("sbuf", [128, 32], "float32"), "ri": ("sbuf", [128, 32], "int32"),
-    "ro": ("sbuf", [128, 22], "uint16"), "gcm": ("sbuf", [128, C], "float32"), "zc": ("sbuf", [128, C], "float32"),
-    "ki": ("sbuf", [128, 22], "int32"), "ko": ("sbuf", [128, 22], "uint16"),
+    "ro": ("sbuf", [128, 22], "uint16"), "gcm": ("sbuf", [128, C], "float16"), "zc": ("sbuf", [128, C], "float16"),
+    "ko": ("sbuf", [128, 22], "uint16"), "kb": ("sbuf", [128, 22], "int32"), "t1": ("sbuf", [128, 22], "float32"), "t2": ("sbuf", [128, 22], "float32"),
+    "yd": ("sbuf", [128, 22], "float32"), "yl": ("sbuf", [128, 22], "float32"), "roe": ("sbuf", [128, 22], "uint16"), "eo": ("sbuf", [128, 22], "uint16"),
+    "lk": ("sbuf", [128, 704], "int32"),
     "ci": ("sbuf", [128, 16], "int32"), "cf": ("sbuf", [128, 16], "float32"), "fw": ("sbuf", [128, 16], "float32"),
     "fc": ("sbuf", [128, 128], "float32"), "c3": ("sbuf", [128, 128], "float32"), "z8": ("sbuf", [128, 8], "float32"),
     "yt": ("sbuf", [128, C], "float32"), "lt": ("sbuf", [128, 704], "float32"),
@@ -41,8 +45,10 @@ for _r in range(3):
     SCRATCH["hs%d" % _r] = ("sbuf", [128, C], "uint8")
     SCRATCH["aq%d" % _r] = ("sbuf", [128, C], F8)
     SCRATCH["as%d" % _r] = ("sbuf", [128, C], "uint8")
+    SCRATCH["ki%d" % _r] = ("sbuf", [128, 22], "int32")
+    SCRATCH["ka%d" % _r] = ("sbuf", [128, 22], "int32")
 SEMAPHORES = (["sv", "ss", "st", "sg", "lu", "lx", "lt", "lid", "lw", "lv", "snt", "outs"]
-              + ["hop%d" % r for r in range(3)] + ["arr%d%d" % (r, c) for r in range(3) for c in range(2)])
+              + [n % r for r in range(3) for n in ("hop%d", "kop%d", "ark%d")] + ["arr%d%d" % (r, c) for r in range(3) for c in range(2)])
 
 
 def rank_program(g, core, T, topo):
@@ -192,8 +198,7 @@ def rank_program(g, core, T, topo):
     ts(T.fc[:, 0:64], T.fc[:, 0:64], F(12), 351.0, A.add, A.min, ["fc", "f12"], ["fca"])
     ts(T.fc[:, 64:128], T.fc[:, 64:128], F(13), 351.0, A.add, A.min, ["fc", "f13"], ["fca"])
     ts(T.c3[:], T.fc[:], 3.0, None, A.mult, None, ["fca"], ["c3"])
-    op("v", V.memset, (T.one[:], 1.0), [], ["one"])
-    op("v", V.memset, (T.lw[:], 0.0), [], ["lwz"])
+    ts(F(4), I(6), 352.0, None, A.mult, None, ["ci6", "f4", "f5"], ["hof"])
     for k, val in ((0, 0), (1, 1), (2, -1)):
         iota(T.d0[:, k:1056:3], [[0, C]], val, 0, ["phi" if k == 1 else "d0c"])
     quant(T.uq[:], T.us[:], T.ut[:], ["ut"], ["uq"])
@@ -215,12 +220,13 @@ def rank_program(g, core, T, topo):
     act(T.d1[:, 1:1056:3], T.d1[:, 1:1056:3], ["d1s"], ["d1m"], scale=1.5)
     act(T.d1[:, 0:1056:3], T.d1[:, 0:1056:3], ["d1d"], ["d1b"], scale=1.5)
     iota(T.rl[:, :], [[0, 2], [96, 16]], -287, 3, ["rli"])
-    before("g", ["lwz"], [])
-    iota(T.lw[0:32, 0:384], [[3, 384]], 1, 0, ["lw"])
+    iota(T.lw[:, :], [[3, 768]], 1, 0, ["lwz"])
+    iota(T.one[:, :], [[0, 512]], 1, 0, ["one"])
     for b in range(4):
         op("g", g.affine_select, (T.et[:, 512 * b:512 * b + 512], T.one[:], [[-1, 512]], A.is_equal, 0.0, b, 4), ["one"], ["et"])
 
-    K12 = (T.ko[:, 0:12], T.ko[:, 12:22])
+    iota(T.lk[:, :], [[0, 704]], 0, 0, ["lkz"], False)
+    K12 = (T.ko[:, 0:CH[0][1] // 16], T.ko[:, CH[0][1] // 16:22])
 
     def plane(t, b, c0=0, c1=C):
         return t[:, C * b + c0:C * b + c1]
@@ -232,20 +238,21 @@ def rank_program(g, core, T, topo):
         partner = T.cores[rank ^ STEP[rnd]]
         if rnd:
             op("s", S.activation, (T.d0[:, 1:1056:3], bank(1), SIGN), ["b1", "f5"], ["phi"], {"bias": 2.0 ** -94, "scale": F(5)})
-        for b in range(4):
-            act(plane(T.xh, b), inter(T.xt, b), ["xt"], ["xh%d" % b], scale=0.5)
-        act(T.xi[:], T.xt[:], ["xt"], ["xi"], scale=0.5)
         ts(T.sb[:], bank(0), 0.0, 1.0, A.is_le, A.add, ["b0"], ["sb"])
         tt(T.gm[:], T.sb[:].indirect(T.sl[:, 8:16]), T.c3[:], A.add, ["sb", "sl", "c3"], ["gm"])
 
         def wrap(src, key, ql, qr):
-            op("v", V.transpose, (T.zt[:], src), [key], ["zt"])
-            tc(T.off[:, 0:4], T.zt[:, ql:64:16], ["zt"], ["off"])
-            tc(T.off[:, 4:8], T.zt[:, 64 + qr:128:16], ["zt"], ["off"])
+            z = "zm" if key == "gm" else "zt"
+            op("v", V.transpose, (T[z][:], src), [key], [z])
+            tc(T.off[:, 0:4], T[z][:, ql:64:16], [z], ["off"])
+            tc(T.off[:, 4:8], T[z][:, 64 + qr:128:16], [z], ["off"])
         wrap(T.gm[:], "gm", 7, 8)
-        tc(T.bra[:], T.sb[:].indirect(T.sl[:, 0:8]), ["sb", "sl"], ["bra"])
+        act(T.bra[:], T.sb[:].indirect(T.sl[:, 0:8]), ["sb", "sl"], ["bra"])
+        act(T.brb[:], T.sb[:].indirect(T.sl[:, 8:16]), ["sb", "sl"], ["brb"])
+        for b in range(4):
+            act(plane(T.xh, b), inter(T.xt, b), ["xt"], ["xh%d" % b], scale=0.5)
+        act(T.xi[:], T.xt[:], ["xt"], ["xi"], scale=0.5)
         op("v", V.tensor_tensor_scan, (T.tw[:], T.d0[:], T.d1[:], 0.0, A.mult, A.add), ["d0c", "phi", "d1b", "d1m", "d1n"], ["tw"])
-        tc(T.brb[:], T.sb[:].indirect(T.sl[:, 8:16]), ["sb", "sl"], ["brb"])
         hop = "hop%d" % rnd
 
         def land(qn, gt, key, lists):
@@ -268,46 +275,69 @@ def rank_program(g, core, T, topo):
                 if t:
                     todo += [("l", 8, t), ("r", 8, 7 - t)]
                 land("y" if t < 6 else "ys", T[name], name, todo)
-        ts(T.ri[:], T.rl[:], -1.5, 1.0 / 3.0, A.add, A.mult, ["rl", "rli"], ["ri"])
         for h in range(2):
-            ts(T.ro[:, h:22:2], T.ri[:, 16 * h:16 * h + 11], 384.0 * h, None, A.add, None, ["ri"], ["ro"])
-        tc(T.gcm[:], T.lw[:].indirect(T.ro[:]), ["lw", "ro"], ["gcm"])
+            ts(T.ro[:, h:22:2], T.rl[:, 16 * h:16 * h + 11], 1152.0 * h - 1.0, 1.0 / 3.0, A.add, A.mult, ["rl", "rli"], ["ro"])
+        tc(T.gcm[:], T.lw[:].indirect(T.ro[:]), ["lw", "lwz", "ro"], ["gcm"])
         op("v", V.transpose, (T.zc[:], T.gcm[:]), ["gcm"], ["zc"])
-        ts(T.ki[:], T.zc[:, 0:352:16], -1.5, 1.0 / 3.0, A.add, A.mult, ["zc"], ["ki"])
-        tc(T.ko[:], T.ki[:], ["ki"], ["ko"])
+        ki, kk = T["ki%d" % rnd], "ki%d" % rnd
+        ts(ki[:], T.zc[:, 0:352:16], -1.0, 1.0 / 3.0, A.add, A.mult, ["zc"], [kk])
+        ts(T.ko[:], T.zc[:, 0:352:16], -1.0, 1.0 / 3.0, A.add, A.mult, ["zc"], ["ko"])
+        rid, pid = topo.addr(partner)[0:2]
+        mask = topo.mask(core, partner)
+        ne = len(topo.engines(core, partner))
+        hq, hs, aq, as_ = T["hq%d" % rnd], T["hs%d" % rnd], T["aq%d" % rnd], T["as%d" % rnd]
+
+        def send(out, in_, sem, key):
+            before("g", [key], [])
+            g.remote_dma(out, in_, T.sem[sem], T.sem.snt, pid, rid, mask)
+            total["snt"] = total.get("snt", 0) + ne
+            total[sem] = total.get(sem, 0) + ne
+
+        def send_h(c):
+            c0, c1 = CH[c]
+            quant(hq[:, c0:c1], hs[:, c0:c1], T.hl[:, 4 * c0:4 * c1], ["hl%d" % c], ["hq%d%d" % (rnd, c)])
+            send(u8(aq[:, c0:c1]), u8(hq[:, c0:c1]), "arr%d%d" % (rnd, c), "hq%d%d" % (rnd, c))
+            send(as_[:, c0:c1], hs[:, c0:c1], "arr%d%d" % (rnd, c), "hq%d%d" % (rnd, c))
+        send(T["ka%d" % rnd][:], ki[:], "ark%d" % rnd, kk)
         for c, (c0, c1) in enumerate(CH):
             for b in range(4):
+                if c == 1 and b == LATE:
+                    send_h(0)
                 tt(inter(T.vt, b, c0, c1), plane(T.xh, b).indirect(K12[c]), inter(T.xi, b, c0, c1), A.add, ["xh%d" % b, "xi", "ko"], ["vt%d" % c])
             quant(T.vq[:, c0:c1], T.vs[:, c0:c1], T.vt[:, 4 * c0:4 * c1], ["vt%d" % c], ["vq%d" % c])
             for b in range(4):
                 mm(4 * c + b, c1 - c0, T.wq[:, 128 * b:128 * b + 128], T.wp[:, 128 * b:128 * b + 128], T.vq[:, c0:c1], T.vs[:, c0:c1], ["wq", "vq%d" % c])
                 if c == 0 or b % 2:
-                    act(plane(T.hp, b, c0, c1), bank(4 * c + b, c1 - c0), ["b%d" % (4 * c + b)], ["hp%d" % b], scale=0.03125)
+                    act(inter(T.hl, b, c0, c1), bank(4 * c + b, c1 - c0), ["b%d" % (4 * c + b)], ["hl%d" % c], scale=0.03125)
+            if c == PLACES:
+                ts(T.kb[:], ki[:], 4, None, SR, None, [kk], ["kb"])
+                ts(T.t1[:], ki[:], 22.0, F(4), A.mult, A.add, [kk, "hof"], ["t1"])
+                ts(T.t2[:], T.kb[:], -351.0, None, A.mult, None, ["kb"], ["t2"])
+                for e in range(2):
+                    tt(T.yd[:, 11 * e:11 * e + 11], T.t1[:, e:22:2], T.t2[:, e:22:2], A.add, ["t1", "t2"], ["yd"])
             if c == 1:
                 for b in (0, 2):
-                    ts(plane(T.hp, b, c0, c1), bank(4 + b, c1 - c0), 0.03125, None, A.mult, None, ["b%d" % (4 + b)], ["hp%d" % b])
-        hq, hs, aq, as_ = T["hq%d" % rnd], T["hs%d" % rnd], T["aq%d" % rnd], T["as%d" % rnd]
-        rid, pid = topo.addr(partner)[0:2]
-        mask = topo.mask(core, partner)
-        ne = len(topo.engines(core, partner))
-        for c, (c0, c1) in enumerate(CH):
-            for b in (1, 3):
-                act(inter(T.hl, b, c0, c1), plane(T.hp, b).indirect(K12[c]), ["hp%d" % b, "ko"], ["hl%d" % c])
-            for b in (0, 2):
-                tc(inter(T.hl, b, c0, c1), plane(T.hp, b).indirect(K12[c]), ["hp%d" % b, "ko"], ["hl%d" % c])
-            quant(hq[:, c0:c1], hs[:, c0:c1], T.hl[:, 4 * c0:4 * c1], ["hl%d" % c], ["hq%d%d" % (rnd, c)])
-            before("g", ["hq%d%d" % (rnd, c)], [])
-            arr = T.sem["arr%d%d" % (rnd, c)]
-            g.remote_dma(u8(aq[:, c0:c1]), u8(hq[:, c0:c1]), arr, T.sem.snt, pid, rid, mask)
-            g.remote_dma(as_[:, c0:c1], hs[:, c0:c1], arr, T.sem.snt, pid, rid, mask)
-            total["snt"] = total.get("snt", 0) + 2 * ne
-            total["arr%d%d" % (rnd, c)] = 2 * ne
+                    ts(inter(T.hl, b, c0, c1), bank(4 + b, c1 - c0), 0.03125, None, A.mult, None, ["b%d" % (4 + b)], ["hl1"])
+                send_h(1)
+        for d in (0, 16):
+            need("y", [("ark%d" % rnd, None)])
+            dma("y", T.lk[d:128:32, :], T["ka%d" % rnd][:], ["lkz"], ["lk"], "kop%d" % rnd)
+        for a in range(4):
+            for h in range(2):
+                for e in range(2):
+                    dma("y", T.yl[32 * a + 16 * e:32 * a + 16 * e + 16, 11 * h:11 * h + 11], T.yd[32 * a + 16 * h:32 * a + 16 * h + 16, 11 * e:11 * e + 11],
+                        ["yd"], ["yl"], "kop%d" % rnd)
         if rnd:
             tt(T.d1[:, 0:1056:3], T.d1[:, 0:1056:3], T.d0[:, 1:1056:3], A.mult, ["d1b", "phi"], ["d1b"])
         else:
             quant(T.eq[:], T.es[:], T.et[:], ["et"], ["eq"])
         if rnd == 2:
             quant(T.zq[:], T.zs[:], T.vv[:], ["vv"], ["zq"])
+        for h in range(2):
+            tc(T.roe[:, h:22:2], T.yl[:, 11 * h:11 * h + 11], ["yl"], ["roe"])
+        tc(T.gcm[:], T.lk[:].indirect(T.roe[:]), ["lk", "lkz", "roe"], ["gcm"])
+        op("v", V.transpose, (T.zc[:], T.gcm[:]), ["gcm"], ["zc"])
+        tc(T.eo[:], T.zc[:, 0:352:16], ["zc"], ["eo"])
         for c, (c0, c1) in enumerate(CH):
             need("t", [("arr%d%d" % (rnd, c), None)])
             for b in range(4):
@@ -317,7 +347,7 @@ def rank_program(g, core, T, topo):
                 else:
                     tc(plane(T.dp, b, c0, c1), bank(4 * c + b, c1 - c0), ["b%d" % (4 * c + b)], ["dp%d" % b])
         for b in (0, 2, 1, 3):
-            tt(inter(T.xt, b), plane(T.dp, b).indirect(T.ko[:]), inter(T.vt, b), A.add, ["dp%d" % b, "ko", "vt0", "vt1"], ["xt"])
+            tt(inter(T.xt, b), plane(T.dp, b).indirect(T.eo[:]), inter(T.vt, b), A.add, ["dp%d" % b, "eo", "vt0", "vt1"], ["xt"])
         quant(T.xq[:], T.xs[:], T.xt[:], ["xt"], ["xq"])
         scores([0, 1] if rnd < 2 else [1])
 
@@ -334,4 +364,4 @@ def rank_program(g, core, T, topo):
     dma("y", T.lr[0:8, 0:704], T.lt[0:8, :], ["lt"], [], "outs")
     dma("s", T.lr[1:8, 704:1408], T.lt[9:16, :], ["lt"], [], "outs")
     dma("s", T.lr[0:1, 704:1408], T.lt[23:24, :], ["lt"], [], "outs")
-    need("g", [(s, None) for s in total if not s.startswith("arr")])
+    need("g", [(s, None) for s in total if not s.startswith("ar")])

@@ -32,8 +32,7 @@ SCRATCH = {
     "off": ("sbuf", [128, 8], "uint16"), "sl": ("sbuf", [128, 16], "uint16"), "ul": ("sbuf", [128, 16], "uint16"),
     "lw": ("sbuf", [128, 768], "float32"), "rl": ("sbuf", [128, 32], "float32"), "ri": ("sbuf", [128, 32], "int32"),
     "ro": ("sbuf", [128, 22], "uint16"), "gcm": ("sbuf", [128, C], "float16"), "zc": ("sbuf", [128, C], "float16"),
-    "ko": ("sbuf", [128, 22], "uint16"), "kb": ("sbuf", [128, 22], "int32"), "t1": ("sbuf", [128, 22], "float32"), "t2": ("sbuf", [128, 22], "float32"),
-    "yd": ("sbuf", [128, 22], "float32"), "yl": ("sbuf", [128, 22], "float32"), "roe": ("sbuf", [128, 22], "uint16"), "eo": ("sbuf", [128, 22], "uint16"),
+    "ko": ("sbuf", [128, 22], "uint16"), "yw": ("sbuf", [128, C], "float32"), "roe": ("sbuf", [128, 22], "uint16"), "eo": ("sbuf", [128, 22], "uint16"),
     "lk": ("sbuf", [128, 704], "int32"),
     "ci": ("sbuf", [128, 16], "int32"), "cf": ("sbuf", [128, 16], "float32"), "fw": ("sbuf", [128, 16], "float32"),
     "fc": ("sbuf", [128, 128], "float32"), "c3": ("sbuf", [128, 128], "float32"), "z8": ("sbuf", [128, 8], "float32"),
@@ -148,14 +147,14 @@ def rank_program(g, core, T, topo):
         kw = {"allow_small_or_imprecise_dtypes": True} if f else {}
         op("g", g.iota, (out, pat, base, cm), [], W, kw)
     iota(T.ci[:, 0:1], [[0, 1]], 0, 1, ["ci0"], False)
+    iota(T.idt[:, :], [[1, 8], [0, 2], [8, 44]], 0, 0, ["idt"], False)
+    dma("y", T.ti[8:128:16, :], T.idt[0:8, :], ["idt"], ["ti"], "lt")
     iota(T.fw[:, 0:4], [[16, 4]], 0, 0, ["fw"])
     iota(T.fw[:, 4:8], [[1, 4]], 0, 0, ["fw"])
     iota(T.fw[:, 8:12], [[32, 2], [48, 2]], 0, 0, ["fw"])
     iota(T.fw[:, 12:16], [[2, 2], [4, 2]], 0, 0, ["fw"])
     iota(T.fc[:, 0:64], [[32, 2], [48, 2], [1, 16]], 0, 0, ["fc"])
     iota(T.fc[:, 64:128], [[2, 2], [4, 2], [32, 16]], 0, 0, ["fc"])
-    iota(T.idt[:, :], [[1, 8], [0, 2], [8, 44]], 0, 0, ["idt"], False)
-    dma("y", T.ti[8:128:16, :], T.idt[0:8, :], ["idt"], ["ti"], "lt")
     op("v", V.memset, (T.z8[:], 0.0), [], ["z8"])
 
     def I(k):
@@ -225,6 +224,7 @@ def rank_program(g, core, T, topo):
     for b in range(4):
         op("g", g.affine_select, (T.et[:, 512 * b:512 * b + 512], T.one[:], [[-1, 512]], A.is_equal, 0.0, b, 4), ["one"], ["et"])
 
+    iota(T.yw[:, :], [[1, 22], [22, 16]], 0, 0, ["yw0"])
     iota(T.lk[:, :], [[0, 704]], 0, 0, ["lkz"], False)
     K12 = (T.ko[:, 0:CH[0][1] // 16], T.ko[:, CH[0][1] // 16:22])
 
@@ -275,6 +275,14 @@ def rank_program(g, core, T, topo):
                 if t:
                     todo += [("l", 8, t), ("r", 8, 7 - t)]
                 land("y" if t < 6 else "ys", T[name], name, todo)
+        if rnd:
+            tt(T.d1[:, 0:1056:3], T.d1[:, 0:1056:3], T.d0[:, 1:1056:3], A.mult, ["d1b", "phi"], ["d1b"])
+        else:
+            quant(T.eq[:], T.es[:], T.et[:], ["et"], ["eq"])
+        if rnd == 2:
+            quant(T.zq[:], T.zs[:], T.vv[:], ["vv"], ["zq"])
+        if rnd == 0:
+            ts(T.yw[:], T.yw[:], F(4), None, A.add, None, ["yw0", "hof"], ["yw"])
         for h in range(2):
             ts(T.ro[:, h:22:2], T.rl[:, 16 * h:16 * h + 11], 1152.0 * h - 1.0, 1.0 / 3.0, A.add, A.mult, ["rl", "rli"], ["ro"])
         tc(T.gcm[:], T.lw[:].indirect(T.ro[:]), ["lw", "lwz", "ro"], ["gcm"])
@@ -310,11 +318,7 @@ def rank_program(g, core, T, topo):
                 if c == 0 or b % 2:
                     act(inter(T.hl, b, c0, c1), bank(4 * c + b, c1 - c0), ["b%d" % (4 * c + b)], ["hl%d" % c], scale=0.03125)
             if c == PLACES:
-                ts(T.kb[:], ki[:], 4, None, SR, None, [kk], ["kb"])
-                ts(T.t1[:], ki[:], 22.0, F(4), A.mult, A.add, [kk, "hof"], ["t1"])
-                ts(T.t2[:], T.kb[:], -351.0, None, A.mult, None, ["kb"], ["t2"])
-                for e in range(2):
-                    tt(T.yd[:, 11 * e:11 * e + 11], T.t1[:, e:22:2], T.t2[:, e:22:2], A.add, ["t1", "t2"], ["yd"])
+                tc(T.gcm[:], T.yw[:].indirect(T.ko[:]), ["yw", "ko"], ["gcm"])
             if c == 1:
                 for b in (0, 2):
                     ts(inter(T.hl, b, c0, c1), bank(4 + b, c1 - c0), 0.03125, None, A.mult, None, ["b%d" % (4 + b)], ["hl1"])
@@ -322,19 +326,8 @@ def rank_program(g, core, T, topo):
         for d in (0, 16):
             need("y", [("ark%d" % rnd, None)])
             dma("y", T.lk[d:128:32, :], T["ka%d" % rnd][:], ["lkz"], ["lk"], "kop%d" % rnd)
-        for a in range(4):
-            for h in range(2):
-                for e in range(2):
-                    dma("y", T.yl[32 * a + 16 * e:32 * a + 16 * e + 16, 11 * h:11 * h + 11], T.yd[32 * a + 16 * h:32 * a + 16 * h + 16, 11 * e:11 * e + 11],
-                        ["yd"], ["yl"], "kop%d" % rnd)
-        if rnd:
-            tt(T.d1[:, 0:1056:3], T.d1[:, 0:1056:3], T.d0[:, 1:1056:3], A.mult, ["d1b", "phi"], ["d1b"])
-        else:
-            quant(T.eq[:], T.es[:], T.et[:], ["et"], ["eq"])
-        if rnd == 2:
-            quant(T.zq[:], T.zs[:], T.vv[:], ["vv"], ["zq"])
-        for h in range(2):
-            tc(T.roe[:, h:22:2], T.yl[:, 11 * h:11 * h + 11], ["yl"], ["roe"])
+        op("v", V.transpose, (T.zc[:], T.gcm[:]), ["gcm"], ["zc"])
+        tc(T.roe[:], T.zc[:, 0:352:16], ["zc"], ["roe"])
         tc(T.gcm[:], T.lk[:].indirect(T.roe[:]), ["lk", "lkz", "roe"], ["gcm"])
         op("v", V.transpose, (T.zc[:], T.gcm[:]), ["gcm"], ["zc"])
         tc(T.eo[:], T.zc[:, 0:352:16], ["zc"], ["eo"])

from concourse.bass import DstId, RemoteDMATransfer
from concourse.mybir import dt, AluOpType, ActivationFunctionType

C = 352
STEP = (1, 2, 4)
CH = ((0, 192), (192, 352))
PLACES = 1
LATE = 3
A = AluOpType
COPY = ActivationFunctionType.Copy
SIGN = ActivationFunctionType.Sign
F8 = "float8_e4m3fn_x4"

SCRATCH = {
    "xt": ("sbuf", [128, 4 * C], "bfloat16"), "xh": ("sbuf", [128, 4 * C], "bfloat16"),
    "vt": ("sbuf", [128, 4 * C], "bfloat16"), "hp": ("sbuf", [128, 4 * C], "bfloat16"),
    "hl": ("sbuf", [128, 4 * C], "bfloat16"), "dp": ("sbuf", [128, 4 * C], "bfloat16"),
    "ut": ("sbuf", [128, 512], "bfloat16"), "vv": ("sbuf", [128, 512], "bfloat16"), "et": ("sbuf", [128, 2048], "bfloat16"),
    "one": ("sbuf", [128, 512], "bfloat16"), "xi": ("sbuf", [128, 4 * C], "bfloat16"),
    "xq": ("sbuf", [128, C], F8), "xs": ("sbuf", [128, C], "uint8"),
    "vq": ("sbuf", [128, C], F8), "vs": ("sbuf", [128, C], "uint8"),
    "uq": ("sbuf", [128, 128], F8), "us": ("sbuf", [128, 128], "uint8"),
    "pq": ("sbuf", [128, 256], F8), "ps": ("sbuf", [128, 256], "uint8"),
    "zq": ("sbuf", [128, 128], F8), "zs": ("sbuf", [128, 128], "uint8"),
    "eq": ("sbuf", [128, 512], F8), "es": ("sbuf", [128, 512], "uint8"),
    "wq": ("sbuf", [128, 512], F8), "wp": ("sbuf", [128, 512], "uint8"),
    "ti": ("sbuf", [128, 704], "int32"), "tf": ("sbuf", [128, 704], "float32"), "idt": ("sbuf", [128, 704], "int32"),
    "d0": ("sbuf", [128, 1056], "float32"), "d1": ("sbuf", [128, 1056], "float32"), "tw": ("sbuf", [128, 1056], "float32"),
    "sb": ("sbuf", [128, C], "float32"), "bra": ("sbuf", [128, 128], "float32"), "brb": ("sbuf", [128, 128], "float32"),
    "gm": ("sbuf", [128, 128], "float16"), "zm": ("sbuf", [128, 128], "float16"), "g0": ("sbuf", [128, 128], "float32"), "g2": ("sbuf", [128, 128], "float32"),
    "g4": ("sbuf", [128, 128], "float32"), "g6": ("sbuf", [128, 128], "float32"), "zt": ("sbuf", [128, 128], "float32"),
    "off": ("sbuf", [128, 8], "uint16"), "sl": ("sbuf", [128, 16], "uint16"), "ul": ("sbuf", [128, 16], "uint16"),
    "lw": ("sbuf", [128, 768], "float32"), "rl": ("sbuf", [128, 32], "float32"), "ri": ("sbuf", [128, 32], "int32"),
    "ro": ("sbuf", [128, 22], "uint16"), "gcm": ("sbuf", [128, C], "float16"), "zc": ("sbuf", [128, C], "float16"),
    "ko": ("sbuf", [128, 22], "uint16"), "yw": ("sbuf", [128, C], "float32"), "roe": ("sbuf", [128, 22], "uint16"), "eo": ("sbuf", [128, 22], "uint16"),
    "lk": ("sbuf", [128, 704], "int32"),
    "ci": ("sbuf", [128, 16], "int32"), "cf": ("sbuf", [128, 16], "float32"), "fw": ("sbuf", [128, 16], "float32"),
    "fc": ("sbuf", [128, 128], "float32"), "c3": ("sbuf", [128, 128], "float32"), "z8": ("sbuf", [128, 8], "float32"),
    "yt": ("sbuf", [128, C], "float32"), "lt": ("sbuf", [128, 704], "float32"),
    "pm": ("psum", [128, 4096], "float32"),
}
for _r in range(3):
    SCRATCH["hq%d" % _r] = ("sbuf", [128, C], F8)
    SCRATCH["hs%d" % _r] = ("sbuf", [128, C], "uint8")
    SCRATCH["aq%d" % _r] = ("sbuf", [128, C], F8)
    SCRATCH["as%d" % _r] = ("sbuf", [128, C], "uint8")
    SCRATCH["ki%d" % _r] = ("sbuf", [128, 22], "int32")
    SCRATCH["ka%d" % _r] = ("sbuf", [128, 22], "int32")
SEMAPHORES = (["sv", "ss", "st", "sg", "lu", "lx", "lt", "lid", "lw", "lv", "snt", "outs"]
              + [n % r for r in range(3) for n in ("hop%d", "kop%d", "ark%d")] + ["arr%d%d" % (r, c) for r in range(3) for c in range(2)])


def rank_program(g, core, T, topo):
    rank = T.rank_of(core)
    if rank is None:
        return
    Q = {"v": g.vector, "s": g.scalar, "t": g.tensor, "g": g, "y": g.sync}
    SEM = {"v": "sv", "s": "ss", "t": "st", "g": "sg"}
    total = {}
    waited = {}
    gens = {}

    def need(qn, toks):
        best = {}
        for s, n in toks:
            n = total[s] if n is None else n
            best[s] = max(best.get(s, 0), n)
        for s, n in best.items():
            if waited.get((qn, s), 0) < n:
                Q[qn].wait_ge(T.sem[s], n)
                waited[(qn, s)] = n

    def before(qn, R, W):
        toks = []
        for k in R:
            toks += gens.setdefault(k, [[], [], []])[1]
        for k in W:
            e = gens.setdefault(k, [[], [], []])
            if e[2]:
                gens[k] = e = [e[1] + e[2], [], []]
            toks += e[0]
        need(qn, toks)

    def after(tok, R, W):
        for k in R:
            gens[k][2].append(tok)
        for k in W:
            gens[k][1].append(tok)

    def op(qn, fn, args, R, W, kw=None):
        before(qn, R, W)
        s = SEM[qn]
        fn(*args, **(kw or {})).then_inc(T.sem[s], 1)
        total[s] = total.get(s, 0) + 1
        after((s, total[s]), R, W)

    def dma(qn, out, in_, R, W, sem):
        before(qn, R, W)
        Q[qn].dma_start(out, in_).then_inc(T.sem[sem], 16)
        total[sem] = total.get(sem, 0) + 16
        after((sem, None), R, W)

    V, S, TE = g.vector, g.scalar, g.tensor

    def ts(out, in0, s1, s2, o0, o1, R, W):
        if o1 is None:
            op("v", V.tensor_scalar, (out, in0, s1, None, o0), R, W)
        else:
            op("v", V.tensor_scalar, (out, in0, s1, s2, o0, o1), R, W)

    def tt(out, a, b, o, R, W):
        op("v", V.tensor_tensor, (out, a, b, o), R, W)

    def tc(out, a, R, W):
        op("v", V.tensor_copy, (out, a), R, W)

    def act(out, a, R, W, **kw):
        op("s", S.activation, (out, a, COPY), R, W, kw)

    def bank(i, n=C):
        return T.pm[:, 512 * i:512 * i + n]

    def mm(i, n, lq, ls, rq, rs, R):
        op("t", TE.matmul_mx, (bank(i, n), lq, ls, rq, rs, True, True), R, ["b%d" % i])

    def quant(q, s, t, R, W):
        op("v", V.quantize_mx, (q, s, t), R, W)

    def u8(v):
        return v.bitcast(dt.uint8)

    dma("s", T.ut[:], T.u[:], [], ["ut"], "lu")
    dma("y", T.xt[:], T.x[:], [], ["xt"], "lx")
    for h in range(8):
        qn = "y" if h % 2 else "s"
        if h == 1:
            dma(qn, T.ti[16:23, :], T.lam[0:112, :], [], ["ti"], "lt")
            dma(qn, T.ti[23:24, :], T.rho[0:16, :], [], ["ti"], "lt")
        else:
            dma(qn, T.ti[16 * h:16 * h + 8, :], T.lam[:], [], ["ti"], "lt")
        dma(qn, T.ti[16 * h + 9:16 * h + 16, :], T.rho[16:128, :], [], ["ti"], "lt")
    dma("s", u8(T.wq[:, :]), T.wc[:], [], ["wq"], "lw")
    dma("s", T.wp[:], T.ws[:], [], ["wq"], "lw")
    dma("s", T.vv[:], T.v[:], [], ["vv"], "lv")

    def iota(out, pat, base, cm, W, f=True):
        kw = {"allow_small_or_imprecise_dtypes": True} if f else {}
        op("g", g.iota, (out, pat, base, cm), [], W, kw)
    iota(T.ci[:, 0:1], [[0, 1]], 0, 1, ["ci0"], False)
    iota(T.idt[:, :], [[1, 8], [0, 2], [8, 44]], 0, 0, ["idt"], False)
    dma("y", T.ti[8:128:16, :], T.idt[0:8, :], ["idt"], ["ti"], "lt")
    iota(T.fw[:, 0:4], [[16, 4]], 0, 0, ["fw"])
    iota(T.fw[:, 4:8], [[1, 4]], 0, 0, ["fw"])
    iota(T.fw[:, 8:12], [[32, 2], [48, 2]], 0, 0, ["fw"])
    iota(T.fw[:, 12:16], [[2, 2], [4, 2]], 0, 0, ["fw"])
    iota(T.fc[:, 0:64], [[32, 2], [48, 2], [1, 16]], 0, 0, ["fc"])
    iota(T.fc[:, 64:128], [[2, 2], [4, 2], [32, 16]], 0, 0, ["fc"])
    op("v", V.memset, (T.z8[:], 0.0), [], ["z8"])

    def I(k):
        return T.ci[:, k:k + 1]

    def F(k):
        return T.cf[:, k:k + 1]
    SR, AND = A.logical_shift_right, A.bitwise_and
    ts(I(1), I(0), 15, None, AND, None, ["ci0"], ["ci1"])
    ts(I(2), I(0), 3, 1, SR, AND, ["ci0"], ["ci2"])
    ts(I(3), I(0), 7, None, AND, None, ["ci0"], ["ci3"])
    ts(I(4), I(0), 4, None, SR, None, ["ci0"], ["ci4"])
    ts(I(5), I(0), 5, None, SR, None, ["ci0"], ["ci5"])
    ts(I(6), I(0), 4, 1, SR, AND, ["ci0"], ["ci6"])
    ts(I(7), I(2), -2, 1, A.mult, A.add, ["ci2"], ["ci7"])
    tt(I(8), I(7), I(1), A.add, ["ci7", "ci1"], ["ci8"])
    ts(I(9), I(8), 7, None, AND, None, ["ci8"], ["ci9"])
    ts(F(0), I(9), 16.0, None, A.mult, None, ["ci9"], ["f0"])
    ts(F(1), I(3), 16.0, 1.0, A.mult, A.add, ["ci3"], ["f1"])
    ts(F(2), I(1), 7.0, -112.0, A.is_equal, A.mult, ["ci1"], ["f2"])
    ts(T.ul[:, 0:8], T.z8[:], F(0), None, A.add, None, ["z8", "f0"], ["ul"])
    ts(T.ul[:, 8:16], T.z8[:], F(1), None, A.add, None, ["z8", "f1"], ["ul"])
    need("v", [("sv", total["sv"])])
    ts(T.ul[:, 9:10], F(2), F(1), None, A.add, None, ["f1", "f2"], ["ul"])
    ts(F(3), I(7), 1.0, None, A.mult, None, ["ci7"], ["f3"])
    ts(F(4), I(0), 23.0, -2.0, A.is_equal, A.mult, ["ci0"], ["f4"])
    tt(F(5), F(3), F(4), A.add, ["f3", "f4"], ["f5"])
    tc(F(6), I(1), ["ci1"], ["f6"])
    ts(F(7), I(1), 32.0, None, A.mult, None, ["ci1"], ["f7"])
    tc(F(8), I(6), ["ci6"], ["f8"])
    ts(F(9), I(4), 48.0, F(6), A.mult, A.add, ["ci4", "f6"], ["f9"])
    ts(F(10), I(4), 4.0, F(7), A.mult, A.add, ["ci4", "f7"], ["f10"])
    ts(F(11), I(6), 16.0, None, A.mult, None, ["ci6"], ["f11"])
    ts(F(12), I(5), 96.0, F(11), A.mult, A.add, ["ci5", "f11"], ["f12"])
    ts(F(13), I(5), 8.0, F(8), A.mult, A.add, ["ci5", "f8"], ["f13"])
    tt(F(14), F(12), F(6), A.add, ["f12", "f6"], ["f14"])
    tt(F(15), F(13), F(7), A.add, ["f13", "f7"], ["f15"])
    for k, f in ((0, 9), (4, 10), (8, 14), (12, 15)):
        ts(T.sl[:, k:k + 4], T.fw[:, k:k + 4], F(f), 351.0, A.add, A.min, ["fw", "f%d" % f], ["sl"])
    ts(T.fc[:, 0:64], T.fc[:, 0:64], F(12), 351.0, A.add, A.min, ["fc", "f12"], ["fca"])
    ts(T.fc[:, 64:128], T.fc[:, 64:128], F(13), 351.0, A.add, A.min, ["fc", "f13"], ["fca"])
    ts(T.c3[:], T.fc[:], 3.0, None, A.mult, None, ["fca"], ["c3"])
    ts(F(4), I(6), 352.0, None, A.mult, None, ["ci6", "f4", "f5"], ["hof"])
    for k, val in ((0, 0), (1, 1), (2, -1)):
        iota(T.d0[:, k:1056:3], [[0, C]], val, 0, ["phi" if k == 1 else "d0c"])
    quant(T.uq[:], T.us[:], T.ut[:], ["ut"], ["uq"])
    op("v", V.tensor_copy, (T.pq[:, 0:256].bitcast(dt.uint32), T.uq[:, 0:128].bitcast(dt.uint32).indirect(T.ul[:, 0:16])), ["uq", "ul"], ["pq"])
    act(T.ps[:, 0:256], T.us[:, 0:128].indirect(T.ul[:, 0:16]), ["uq", "ul"], ["pq"])
    quant(T.xq[:], T.xs[:], T.xt[:], ["xt"], ["xq"])

    def scores(rows):
        for k in rows:
            mm(k, C, T.pq[:, 128 * k:128 * k + 128], T.ps[:, 128 * k:128 * k + 128], T.xq[:], T.xs[:], ["pq", "xq"])
    scores([0])
    for r in range(8):
        e, o = T.ti[:, 88 * r:88 * r + 44], T.ti[:, 88 * r + 44:88 * r + 88]
        tt(T.d1[:, 3 * r + 1:1056:24], o, e, A.add, ["ti"], ["d1s"])
    for r in range(8):
        e, o = T.ti[:, 88 * r:88 * r + 44], T.ti[:, 88 * r + 44:88 * r + 88]
        tt(T.d1[:, 3 * r:1056:24], o, e, A.subtract, ["ti"], ["d1d"])
    act(T.d1[:, 2:1056:3], T.d1[:, 1:1056:3], ["d1s"], ["d1n"], scale=3.0)
    act(T.d1[:, 1:1056:3], T.d1[:, 1:1056:3], ["d1s"], ["d1m"], scale=1.5)
    act(T.d1[:, 0:1056:3], T.d1[:, 0:1056:3], ["d1d"], ["d1b"], scale=1.5)
    iota(T.rl[:, :], [[0, 2], [96, 16]], -287, 3, ["rli"])
    iota(T.lw[:, :], [[3, 768]], 1, 0, ["lwz"])
    iota(T.one[:, :], [[0, 512]], 1, 0, ["one"])
    for b in range(4):
        op("g", g.affine_select, (T.et[:, 512 * b:512 * b + 512], T.one[:], [[-1, 512]], A.is_equal, 0.0, b, 4), ["one"], ["et"])

    iota(T.yw[:, :], [[1, 22], [22, 16]], 0, 0, ["yw0"])
    iota(T.lk[:, :], [[0, 704]], 0, 0, ["lkz"], False)
    K12 = (T.ko[:, 0:CH[0][1] // 16], T.ko[:, CH[0][1] // 16:22])

    def plane(t, b, c0=0, c1=C):
        return t[:, C * b + c0:C * b + c1]

    def inter(t, b, c0=0, c1=C):
        return t[:, 4 * c0 + b:4 * c1:4]

    for rnd in range(3):
        partner = T.cores[rank ^ STEP[rnd]]
        if rnd:
            op("s", S.activation, (T.d0[:, 1:1056:3], bank(1), SIGN), ["b1", "f5"], ["phi"], {"bias": 2.0 ** -94, "scale": F(5)})
        ts(T.sb[:], bank(0), 0.0, 1.0, A.is_le, A.add, ["b0"], ["sb"])
        tt(T.gm[:], T.sb[:].indirect(T.sl[:, 8:16]), T.c3[:], A.add, ["sb", "sl", "c3"], ["gm"])

        def wrap(src, key, ql, qr):
            z = "zm" if key == "gm" else "zt"
            op("v", V.transpose, (T[z][:], src), [key], [z])
            tc(T.off[:, 0:4], T[z][:, ql:64:16], [z], ["off"])
            tc(T.off[:, 4:8], T[z][:, 64 + qr:128:16], [z], ["off"])
        wrap(T.gm[:], "gm", 7, 8)
        act(T.bra[:], T.sb[:].indirect(T.sl[:, 0:8]), ["sb", "sl"], ["bra"])
        act(T.brb[:], T.sb[:].indirect(T.sl[:, 8:16]), ["sb", "sl"], ["brb"])
        for b in range(4):
            act(plane(T.xh, b), inter(T.xt, b), ["xt"], ["xh%d" % b], scale=0.5)
        act(T.xi[:], T.xt[:], ["xt"], ["xi"], scale=0.5)
        op("v", V.tensor_tensor_scan, (T.tw[:], T.d0[:], T.d1[:], 0.0, A.mult, A.add), ["d0c", "phi", "d1b", "d1m", "d1n"], ["tw"])
        hop = "hop%d" % rnd

        def land(qn, gt, key, lists):
            for kind, q, to in lists:
                a, h = to // 2, to % 2
                if kind == "l":
                    for d in (0, 16):
                        dma(qn[0], T.lw[32 * a + d:32 * a + d + 1, 384 * h:384 * h + 384], gt[q:128:16, 0:48], [key, "lwz"], ["lw"], hop)
                        qn = qn[1:] + qn[:1]
                else:
                    dma(qn[0], T.rl[32 * a:32 * a + 32, 16 * h:16 * h + 16], gt[q:128:16, 64:128], [key, "rli"], ["rl"], hop)
                    qn = qn[1:] + qn[:1]
        for t in range(7):
            name = "gm" if t % 2 else "g%d" % t
            tt(T[name][:], T.tw[:].indirect(T.off[:, 0:8]), (T.brb if t % 2 else T.bra)[:], A.add, ["tw", "off", "brb" if t % 2 else "bra"], [name])
            if t < 6:
                wrap(T[name][:], name, t, 15 - t)
            if t % 2 == 0:
                todo = [("l", t, t + 1), ("r", 15 - t, 6 - t)]
                if t:
                    todo += [("l", 8, t), ("r", 8, 7 - t)]
                land("y" if t < 6 else "ys", T[name], name, todo)
        if rnd:
            tt(T.d1[:, 0:1056:3], T.d1[:, 0:1056:3], T.d0[:, 1:1056:3], A.mult, ["d1b", "phi"], ["d1b"])
        else:
            quant(T.eq[:], T.es[:], T.et[:], ["et"], ["eq"])
        if rnd == 2:
            quant(T.zq[:], T.zs[:], T.vv[:], ["vv"], ["zq"])
        if rnd == 0:
            ts(T.yw[:], T.yw[:], F(4), None, A.add, None, ["yw0", "hof"], ["yw"])
        for h in range(2):
            ts(T.ro[:, h:22:2], T.rl[:, 16 * h:16 * h + 11], 1152.0 * h - 1.0, 1.0 / 3.0, A.add, A.mult, ["rl", "rli"], ["ro"])
        tc(T.gcm[:], T.lw[:].indirect(T.ro[:]), ["lw", "lwz", "ro"], ["gcm"])
        op("v", V.transpose, (T.zc[:], T.gcm[:]), ["gcm"], ["zc"])
        ki, kk = T["ki%d" % rnd], "ki%d" % rnd
        ts(ki[:], T.zc[:, 0:352:16], -1.0, 1.0 / 3.0, A.add, A.mult, ["zc"], [kk])
        ts(T.ko[:], T.zc[:, 0:352:16], -1.0, 1.0 / 3.0, A.add, A.mult, ["zc"], ["ko"])
        rid, pid = topo.addr(partner)[0:2]
        mask = topo.mask(core, partner)
        ne = len(topo.engines(core, partner))
        hq, hs, aq, as_ = T["hq%d" % rnd], T["hs%d" % rnd], T["aq%d" % rnd], T["as%d" % rnd]

        def send(out, in_, sem, key):
            before("g", [key], [])
            g.remote_dma(out, in_, T.sem[sem], T.sem.snt, pid, rid, mask)
            total["snt"] = total.get("snt", 0) + ne
            total[sem] = total.get(sem, 0) + ne

        def send_h(c):
            c0, c1 = CH[c]
            quant(hq[:, c0:c1], hs[:, c0:c1], T.hl[:, 4 * c0:4 * c1], ["hl%d" % c], ["hq%d%d" % (rnd, c)])
            send(u8(aq[:, c0:c1]), u8(hq[:, c0:c1]), "arr%d%d" % (rnd, c), "hq%d%d" % (rnd, c))
            send(as_[:, c0:c1], hs[:, c0:c1], "arr%d%d" % (rnd, c), "hq%d%d" % (rnd, c))
        send(T["ka%d" % rnd][:], ki[:], "ark%d" % rnd, kk)
        for c, (c0, c1) in enumerate(CH):
            for b in range(4):
                if c == 1 and b == LATE:
                    send_h(0)
                tt(inter(T.vt, b, c0, c1), plane(T.xh, b).indirect(K12[c]), inter(T.xi, b, c0, c1), A.add, ["xh%d" % b, "xi", "ko"], ["vt%d" % c])
            quant(T.vq[:, c0:c1], T.vs[:, c0:c1], T.vt[:, 4 * c0:4 * c1], ["vt%d" % c], ["vq%d" % c])
            for b in range(4):
                mm(4 * c + b, c1 - c0, T.wq[:, 128 * b:128 * b + 128], T.wp[:, 128 * b:128 * b + 128], T.vq[:, c0:c1], T.vs[:, c0:c1], ["wq", "vq%d" % c])
                if c == 0 or b % 2:
                    act(inter(T.hl, b, c0, c1), bank(4 * c + b, c1 - c0), ["b%d" % (4 * c + b)], ["hl%d" % c], scale=0.03125)
            if c == PLACES:
                tc(T.gcm[:], T.yw[:].indirect(T.ko[:]), ["yw", "ko"], ["gcm"])
            if c == 1:
                for b in (0, 2):
                    ts(inter(T.hl, b, c0, c1), bank(4 + b, c1 - c0), 0.03125, None, A.mult, None, ["b%d" % (4 + b)], ["hl1"])
                send_h(1)
        for d in (0, 16):
            need("y", [("ark%d" % rnd, None)])
            dma("y", T.lk[d:128:32, :], T["ka%d" % rnd][:], ["lkz"], ["lk"], "kop%d" % rnd)
        op("v", V.transpose, (T.zc[:], T.gcm[:]), ["gcm"], ["zc"])
        tc(T.roe[:], T.zc[:, 0:352:16], ["zc"], ["roe"])
        tc(T.gcm[:], T.lk[:].indirect(T.roe[:]), ["lk", "lkz", "roe"], ["gcm"])
        op("v", V.transpose, (T.zc[:], T.gcm[:]), ["gcm"], ["zc"])
        tc(T.eo[:], T.zc[:, 0:352:16], ["zc"], ["eo"])
        for c, (c0, c1) in enumerate(CH):
            need("t", [("arr%d%d" % (rnd, c), None)])
            for b in range(4):
                mm(4 * c + b, c1 - c0, T.eq[:, 128 * b:128 * b + 128], T.es[:, 128 * b:128 * b + 128], aq[:, c0:c1], as_[:, c0:c1], ["eq"])
                if c == 0 or b % 2:
                    act(plane(T.dp, b, c0, c1), bank(4 * c + b, c1 - c0), ["b%d" % (4 * c + b)], ["dp%d" % b])
                else:
                    tc(plane(T.dp, b, c0, c1), bank(4 * c + b, c1 - c0), ["b%d" % (4 * c + b)], ["dp%d" % b])
        for b in (0, 2, 1, 3):
            tt(inter(T.xt, b), plane(T.dp, b).indirect(T.eo[:]), inter(T.vt, b), A.add, ["dp%d" % b, "eo", "vt0", "vt1"], ["xt"])
        quant(T.xq[:], T.xs[:], T.xt[:], ["xt"], ["xq"])
        scores([0, 1] if rnd < 2 else [1])

    mm(2, C, T.zq[:], T.zs[:], T.xq[:], T.xs[:], ["zq", "xq"])
    dma("y", T.oc[:], u8(T.xq[:, :]), ["xq"], [], "outs")
    for k in range(4):
        dma("y", T.osc[4 * k:4 * k + 4, :], T.xs[32 * k:32 * k + 4, :], ["xq"], [], "outs")
    op("s", S.activation, (T.d0[:, 1:1056:3], bank(1), SIGN), ["b1", "f5"], ["phi"], {"bias": 2.0 ** -94, "scale": F(5)})
    tc(T.yt[:], bank(2), ["b2"], ["yt"])
    dma("y", T.y[:], T.yt[:], ["yt"], [], "outs")
    op("v", V.tensor_tensor_scan, (T.tw[:], T.d0[:], T.d1[:], 0.0, A.mult, A.add), ["d0c", "phi", "d1b", "d1m", "d1n"], ["tw"])
    ts(T.lt[:, 0:704:2], T.tw[:, 2:1056:3], 1.0 / 3.0, None, A.mult, None, ["tw"], ["lt"])
    act(T.lt[:, 1:704:2], T.tw[:, 1:1056:3], ["tw"], ["lt"], scale=1.0 / 3.0)
    dma("y", T.lr[0:8, 0:704], T.lt[0:8, :], ["lt"], [], "outs")
    dma("s", T.lr[1:8, 704:1408], T.lt[9:16, :], ["lt"], [], "outs")
    dma("s", T.lr[0:1, 704:1408], T.lt[23:24, :], ["lt"], [], "outs")
    need("g", [(s, None) for s in total if not s.startswith("ar")])
